import numpy as np, ml_dtypes
CORES = [40,41,42,43,44,45,46,47]
N = 8
import mx_ref
BF = ml_dtypes.bfloat16
def entries(a):
    return np.ascontiguousarray(a.T).reshape(-1)
def table(e):
    return np.ascontiguousarray(np.reshape(e, (-1, 16)).T).astype(np.int32)
def cols(t, e):
    v = np.concatenate([t.reshape(128, -1, 4), np.zeros((128, 1, 4), BF)], axis=1)
    return np.ascontiguousarray(v[:, e]).reshape(128, -1)
def f(rng, *shape):
    return mx_ref.flush((rng.standard_normal(shape, dtype=np.float32) * np.exp2(rng.integers(-2, 3, shape[:-1] + (1,)))).astype(BF))
def wide(rng, *shape, cols=0):
    v = rng.standard_normal(shape, dtype=np.float32) * np.exp2(rng.integers(-12, 13, shape)).astype(np.float32)
    if cols: v *= np.repeat(np.exp2(rng.integers(-cols, cols + 1, shape[:-2] + (1, shape[-1] // 4))) * (rng.random(shape[:-2] + (1, shape[-1] // 4)) > 0.0625), 4, axis=-1).astype(np.float32)
    return mx_ref.flush(v.astype(BF))
T, S, CAPP, CL, K, O = 256, 256, 48, 48, 1024, 2
H = 65536 // (N * K)
def counts(rng, tot, cap, lead=None, least=2):
    n = np.full(N, least)
    if lead is not None:
        for i in range(N):
            q = (lead + i) % N; n[q] += min(cap - n[q], tot - n.sum())
    while n.sum() < tot:
        q = rng.integers(0, N)
        if n[q] < cap: n[q] += 1
    return n
def lists(rng, full=False, hot=False, other=False, few=False):
    a, b = rng.integers(1, N, 2); z = rng.integers(0, N); least = 0 if full else 2
    n = np.stack([counts(rng, T, CAPP, (r + a) % N if full or other else z if hot else None, least) for r in range(N)])
    part, pool = [], []
    for q in range(N):
        c = n[:, q].sum(); p = rng.permutation(K)[:c]
        key = q + N * (p + K * rng.integers(0, H, c))
        part.append(np.split(key, np.cumsum(n[:, q])[:-1])); pool.append(rng.choice(key, 1) if few else key)
    has = [np.concatenate([part[q][r] for q in range(N)]) for r in range(N)]
    ky, lk = [], []
    for r in range(N):
        ky.append(table(rng.permutation(has[r])))
        if other:
            s = (r + a) % N; e = rng.permutation(has[s])[:S]; m = np.bincount(e & (N - 1), minlength=N); e = [e]
            for q in ((s + a) % N, (s + a + 1) % N):
                more = rng.permutation(np.setdiff1d(pool[q], part[q][s]))[:CL - m[q]]
                e.append(more); m[q] += len(more)
            while m.sum() < S:
                q = rng.integers(0, N)
                if m[q] < CL: m[q] += 1; e.append(rng.choice(part[q][s], 1))
            u = np.unique(np.concatenate(e)); lead = part[(s + a) % N][s]
            assert len(lead) == CAPP and np.isin(lead, u).all()
            assert any(q != r and m[q] == CL and ((u & (N - 1)) == q).sum() == CL for q in range(N))
        else:
            m = counts(rng, S, CL, (r + b) % N if full else z if hot else None, least)
            e = [rng.choice(pool[q], m[q]) for q in range(N)]
        lk.append(table(rng.permutation(np.concatenate(e))))
    return {"ky": np.stack(ky), "lk": np.stack(lk)}
def setup_inputs(rng):
    d = lists(rng)
    return {"x": f(rng, N, 128, 4 * T), "ky": d["ky"], "lk": d["lk"], "w": f(rng, N, 128, 512 * O)}
def setup_inputs_full(rng):
    return {**setup_inputs(rng), **lists(rng, full=True)}
def setup_inputs_hot(rng):
    return {**setup_inputs(rng), **lists(rng, hot=True)}
def setup_inputs_other(rng):
    return {**setup_inputs(rng), **lists(rng, other=True)}
def setup_inputs_repeats(rng):
    return {**setup_inputs(rng), **lists(rng, few=True)}
def setup_inputs_spread(rng):
    d = setup_inputs(rng); d["x"] = wide(rng, N, 128, 4 * T, cols=8); return d
def check_inputs(d):
    b = []
    keys = np.stack([entries(d["ky"][r]) for r in range(N)]).astype(np.int64)
    if keys.min() < 0 or keys.max() > 65535: b.append("ky")
    if len(np.unique(keys & (N * K - 1))) != N * T: b.append("owner and place")
    for r in range(N):
        l = entries(d["lk"][r]).astype(np.int64)
        if np.bincount(keys[r] & (N - 1), minlength=N).max() > CAPP: b.append("CAPP")
        if not np.isin(l, keys).all(): b.append("lk")
        if np.bincount(l & (N - 1), minlength=N).max() > CL: b.append("CL")
    return b
def reference(x, ky, lk, w):
    every = np.concatenate([x[r] for r in range(N)], axis=1)
    number = np.full(65536, -1); number[np.concatenate([entries(ky[r]) for r in range(N)])] = np.arange(N * T)
    y = np.zeros((N, 128, O * S), np.float32)
    for r in range(N):
        v = mx_ref.quantize(cols(every, number[entries(lk[r])]))
        for o in range(O): y[r][:, S * o:S * o + S] = mx_ref.matmul(mx_ref.quantize(np.ascontiguousarray(w[r][:, 512 * o:512 * o + 512])), v)
    return {"y": y}

@@ -1,0 +1,318 @@
+from concourse.bass import DstId, RemoteDMATransfer
+from concourse.mybir import dt, AluOpType, ActivationFunctionType
+
+N, S, CAP, K, O = 8, 256, 48, 1024, 2
+SL = N * CAP
+HALF = SL // 2
+TAB = K + SL
+F8, F32, BF, I32, U16 = "float8_e4m3fn_x4", "float32", "bfloat16", "int32", "uint16"
+
+SCRATCH = {
+    "xb": ("sbuf", [128, 4 * S], BF), "wb": ("sbuf", [128, 512 * O], BF),
+    "xq": ("sbuf", [128, S], F8), "xs": ("sbuf", [128, S], "uint8"),
+    "wq": ("sbuf", [128, 128 * O], F8), "ws": ("sbuf", [128, 128 * O], "uint8"),
+    "kx": ("sbuf", [128, 64], I32), "ko": ("sbuf", [128, 64], I32), "kt": ("sbuf", [128, 64], I32),
+    "kf": ("sbuf", [128, 256], I32), "pl": ("sbuf", [128, 256], I32),
+    "pio": ("sbuf", [128, 4], I32), "two": ("sbuf", [128, 4], I32), "kf0": ("sbuf", [128, 128], I32),
+    "cq": ("sbuf", [128, 64], F32), "m64": ("sbuf", [128, 64], F32), "sv0": ("sbuf", [128, HALF], F32),
+    "sv": ("sbuf", [128, HALF], BF), "hh": ("sbuf", [128, 4], I32), "h3": ("sbuf", [128, 4], I32),
+    "p31": ("sbuf", [128, 4], I32), "c4": ("sbuf", [128, 4], I32), "c64": ("sbuf", [128, 4], U16),
+    "ev": ("sbuf", [128, 1], F32), "od": ("sbuf", [128, 1], F32), "h8": ("sbuf", [128, 1], F32),
+    "h192": ("sbuf", [128, 1], F32), "ini": ("sbuf", [128, 1], F32), "zz": ("sbuf", [128, 256], BF),
+    "win_k": ("sbuf", [128, SL], F32), "win_l": ("sbuf", [128, SL], F32),
+    "d_k": ("sbuf", [128, 24, 32], "float16"), "t_k": ("sbuf", [128, 24, 32], "float16"),
+    "d_l": ("sbuf", [128, 24, 32], F32), "t_l": ("sbuf", [128, 24, 32], F32),
+    "mn": ("sbuf", [128, 24, 2], F32), "co": ("sbuf", [128, 24], U16),
+    "ks": ("sbuf", [128, 24], F32), "rs": ("sbuf", [128, 24], F32),
+    "x2": ("sbuf", [128, 32], BF), "x2t": ("sbuf", [128, 32], BF), "fof": ("sbuf", [128, 16], F32), "fo": ("sbuf", [128, 16], U16),
+    "kl": ("sbuf", [128, 8, 4], F32), "rl": ("sbuf", [128, 8, 4], F32),
+    "ka": ("sbuf", [128, 4, 3], F32), "kofs": ("sbuf", [128, 12], U16), "rofs": ("sbuf", [128, 48], U16),
+    "tab": ("sbuf", [128, TAB], BF), "d_s": ("sbuf", [128, 2 * SL], BF), "t_s": ("sbuf", [128, 2 * SL], BF),
+    "sg": ("sbuf", [128, 24], F32), "so": ("sbuf", [128, 24], U16),
+    "pk_q": ("sbuf", [128, SL], F8), "pk_s": ("sbuf", [128, SL], "uint8"),
+    "in_q": ("sbuf", [128, SL], F8), "in_s": ("sbuf", [128, SL], "uint8"),
+    "p2_q": ("sbuf", [128, SL], F8), "p2_s": ("sbuf", [128, SL], "uint8"),
+    "bk_q": ("sbuf", [128, SL], F8), "bk_s": ("sbuf", [128, SL], "uint8"),
+    "fp_q": ("sbuf", [128, S], F8), "fp_s": ("sbuf", [128, S], "uint8"),
+    "ps": ("psum", [128, 2048], F32), "yb": ("sbuf", [128, S * O], F32),
+}
+for _c in "kl":
+    SCRATCH["e_" + _c] = ("sbuf", [128, 256], BF)
+    SCRATCH["ef_" + _c] = ("sbuf", [128, 256], BF)
+    SCRATCH["cu_" + _c] = ("sbuf", [128, 256], BF)
+    SCRATCH["ct_" + _c] = ("sbuf", [128, 256], BF)
+    SCRATCH["pr_" + _c] = ("sbuf", [128, 64], F32)
+    SCRATCH["rk_" + _c] = ("sbuf", [128, 64], F32)
+    SCRATCH["po_" + _c] = ("sbuf", [128, 8], U16)
+SEMAPHORES = ["v", "a", "t", "gi", "ld_x", "ld_w", "ld_t", "ld_k", "ld_l", "kin", "rin", "q1", "s1", "q2", "s2",
+              "own1", "own2", "out", "st"]
+
+
+def rank_program(g, core, T, topo):
+    me = T.rank_of(core)
+    if me is None:
+        return
+    A = AluOpType
+    COPY = ActivationFunctionType.Copy
+    vec, act, ten, syn, sem = g.vector, g.scalar, g.tensor, g.sync, T.sem
+    nv, na, seen = [0], [0], {}
+
+    def V(ins):
+        ins.then_inc(sem.v, 1)
+        nv[0] += 1
+        return nv[0]
+
+    def C(ins):
+        ins.then_inc(sem.a, 1)
+        na[0] += 1
+        return na[0]
+
+    def W(q, name, s, k):
+        if seen.get((name, s), 0) < k:
+            q.wait_ge(sem[s], k)
+            seen[(name, s)] = k
+
+    def vw(k, s="v"):
+        W(vec, "v", s, k)
+
+    def aw(k, s="a"):
+        W(act, "a", s, k)
+
+    def sw(k, s):
+        W(syn, "s", s, k)
+
+    def gw(k, s):
+        W(g, "g", s, k)
+
+    near, far = 0, 0
+    dests = []
+    for i in range(1, N):
+        q = (me + i) % N
+        dst = T.cores[q]
+        eng = topo.engines(core, dst)
+        if topo.die(dst) == topo.die(core):
+            pick = eng[0::2][2 * near:2 * near + 2]
+            near += 1
+        else:
+            pick = eng[1::2][2 * far:2 * far + 2]
+            far += 1
+        rid, pid, _ = topo.addr(dst)
+        dests.append((q, DstId(rid=rid, pnc=pid), sum(1 << e for e in pick)))
+    EACH = 2 * (N - 1)
+
+    def send(src, dst, s):
+        g.remote_dma_fused([RemoteDMATransfer(dst_ids=[d], dma_engine_mask=m, remote_sem=sem[s], src=src(q), dst=dst)
+                            for q, d, m in dests], local_sem=sem.out)
+
+    act.dma_start(T.xb[:], T.x[:]).then_inc(sem.ld_x, 16)
+    i_kx = V(vec.memset(T.kx[:], 0))
+    sw(i_kx, "v")
+    aw(i_kx, "v")
+    for src, c0 in ((T.ky, 0), (T.lk, 32)):
+        for b in range(4):
+            (syn if b < 2 else act).dma_start(T.kx[32 * b:32 * b + 8, c0:c0 + 32], src[:]).then_inc(sem.ld_t, 16)
+
+    g.iota(T.kf0[:], [[16, 8], [128, 16]], 0, 0).then_inc(sem.gi, 1)
+    g.iota(T.pio[:], [[0, 4]], 0, 1).then_inc(sem.gi, 1)
+    g.iota(T.two[:], [[2, 4]], 0, 0).then_inc(sem.gi, 1)
+    g.iota(T.cq[:], [[0, 8], [1, 8]], 0, 0, allow_small_or_imprecise_dtypes=True).then_inc(sem.gi, 1)
+    g.iota(T.win_k[:], [[0, 8], [1, CAP]], K + CAP * me, 0, allow_small_or_imprecise_dtypes=True).then_inc(sem.gi, 1)
+    g.iota(T.sv0[:], [[1, HALF]], -HALF, 0, allow_small_or_imprecise_dtypes=True).then_inc(sem.gi, 1)
+    V(vec.memset(T.kf[:, 128:256], 0))
+    vw(2, "gi")
+    i_hh = V(vec.tensor_scalar(T.hh[:], T.pio[:], 4, 1, A.logical_shift_right, A.bitwise_and))
+    i_h3 = V(vec.tensor_scalar(T.h3[:], T.pio[:], 3, 1, A.logical_shift_right, A.bitwise_and))
+    i_31 = V(vec.tensor_scalar(T.p31[:], T.pio[:], 31, None, A.bitwise_and))
+    vw(i_hh)
+    i_h8 = V(vec.tensor_scalar(T.h8[:], T.hh[:, 0:1], 8.0, None, A.mult))
+    vw(i_h8)
+    i_kf = V(vec.tensor_scalar(T.kf[:, 0:128], T.kf0[:], T.h8[:, 0:1], None, A.add))
+    sw(i_kf, "v")
+    aw(i_kf, "v")
+    for src, c0, s in ((T.ky, 0, "ld_k"), (T.lk, 128, "ld_l")):
+        for b in range(4):
+            for h in range(2):
+                p = 32 * b + 16 * h + 1
+                (syn if b < 2 else act).dma_start(T.kf[p:p + 1, c0:c0 + 128], src[h:16:2, :]).then_inc(sem[s], 16)
+    syn.dma_start(T.wb[:], T.w[:]).then_inc(sem.ld_w, 16)
+    vw(3, "gi")
+    vw(i_31)
+    i = V(vec.tensor_tensor(T.c4[:], T.h3[:], T.two[:], A.add))
+    i_ini = V(vec.tensor_scalar(T.ini[:], T.p31[:, 0:1], 12.0, -193.0, A.mult, A.add))
+    i_od = V(vec.tensor_copy(T.od[:], T.hh[:, 0:1]))
+    i_ev = V(vec.tensor_scalar(T.ev[:], T.hh[:, 0:1], -1.0, 1.0, A.mult, A.add))
+    vw(i)
+    i_c64 = V(vec.tensor_copy(T.c64[:], T.c4[:]))
+    vw(4, "gi")
+    i_m64 = V(vec.tensor_scalar(T.m64[:], T.cq[:], 1.0, None, A.min))
+    V(vec.memset(T.e_k[:], 0.0))
+    V(vec.memset(T.e_l[:], 0.0))
+    V(vec.memset(T.zz[:], 0.0))
+    V(vec.tensor_scalar(T.h192[:], T.hh[:, 0:1], float(HALF), None, A.mult))
+    i_con = V(vec.memset(T.win_l[:], float(K)))
+
+    vw(i_con)
+    vw(128, "ld_t")
+    i = V(vec.tensor_scalar(T.ko[:], T.kx[:], N - 1, None, A.bitwise_and))
+    vw(i)
+    i = V(vec.transpose(T.kt[:], T.ko[:]))
+    vw(i)
+    kl = ("k", "l")
+    last = {}
+    for c, w0 in (("k", 0), ("l", 32)):
+        last[c] = V(vec.tensor_tensor(T["e_" + c][:, 0:256:4], T.kt[:, w0:w0 + 8].indirect(T.c64[:, 0:4]), T.cq[:], A.is_equal))
+    for c in kl:
+        vw(last[c])
+        last[c] = V(vec.transpose(T["ef_" + c][:], T["e_" + c][:]))
+    for c in kl:
+        vw(last[c])
+        last[c] = V(vec.tensor_tensor_scan(T["cu_" + c][:], T["ef_" + c][:], T.zz[:], T.ini[:, 0:1], A.add, A.add))
+    for c in kl:
+        vw(last[c])
+        last[c] = V(vec.transpose(T["ct_" + c][:], T["cu_" + c][:]))
+    for c in kl:
+        vw(last[c])
+        last[c] = V(vec.tensor_tensor(T["pr_" + c][:], T["e_" + c][:, 0:256:4], T["ct_" + c][:, 0:256:4], A.mult))
+    for c in kl:
+        vw(last[c])
+        last[c] = V(vec.tensor_tensor_scan(T["rk_" + c][:], T.m64[:], T["pr_" + c][:], 0.0, A.mult, A.add))
+    vw(128, "ld_k")
+    i_plk = V(vec.tensor_scalar(T.pl[:, 0:128], T.kf[:, 0:128], 3, K - 1, A.logical_shift_right, A.bitwise_and))
+    i_rkl = last["l"]
+    for c in kl:
+        vw(last[c])
+        last[c] = V(vec.tensor_scalar(T["po_" + c][:], T["rk_" + c][:, 7:64:8], float(HALF), None, A.add))
+    vw(128, "ld_l")
+    i_pll = V(vec.tensor_scalar(T.pl[:, 128:256], T.kf[:, 128:256], 3, K - 1, A.logical_shift_right, A.bitwise_and))
+
+    vw(5, "gi")
+    vw(last["k"])
+    i_sk = V(vec.tensor_copy(T.win_k[:, 0:SL].indirect(T.po_k[:, 0:8]), T.pl[:, 0:128]))
+    vw(i_pll)
+    i_sl = V(vec.tensor_copy(T.win_l[:, 0:SL].indirect(T.po_l[:, 0:8]), T.pl[:, 128:256]))
+    aw(i_sl, "v")
+    C(act.activation(T.d_l[:, :, 0:16], T.win_l[:], COPY))
+    a_dl = C(act.activation(T.d_l[:, :, 16:32], T.win_l[:], COPY))
+    vw(i_sk)
+    i = V(vec.tensor_copy(T.d_k[:, :, 0:16], T.win_k[:]))
+    vw(i)
+    i = V(vec.tensor_copy(T.d_k[:, :, 16:32], T.d_k[:, :, 0:16]))
+    vw(i)
+    i = V(vec.transpose(T.t_k[:], T.d_k[:]))
+    vw(i)
+    i = V(vec.tensor_tensor(T.mn[:], T.t_k[:, :, 0:2], T.t_k[:, :, 16:18], A.min))
+    vw(i)
+    i_ks = V(vec.tensor_scalar(T.ks[:], T.mn[:, :, 1], (T.ev if me < N // 2 else T.od)[:, 0:1], None, A.mult))
+    i_co = V(vec.tensor_scalar(T.co[:], T.mn[:, :, 0], float(S - 1), None, A.min))
+    gw(i_ks, "v")
+    send(lambda q: T.ks[:, 3 * q:3 * q + 3], T.kl[:, me, 0:3], "kin")
+    vw(16, "ld_x")
+    i_xq = V(vec.quantize_mx(T.xq[:], T.xs[:], T.xb[:]))
+    vw(a_dl, "a")
+    i = V(vec.transpose(T.t_l[:], T.d_l[:]))
+    aw(i_xq, "v")
+    a_pk = C(act.activation(T.pk_s[:, 0:SL], T.xs[:, 0:S].indirect(T.co[:, 0:24]), COPY))
+    vw(i)
+    i_rs = V(vec.tensor_tensor(T.rs[:], T.t_l[:, :, 1], T.t_l[:, :, 17], A.min))
+    gw(i_rs, "v")
+    send(lambda q: T.rs[:, 3 * q:3 * q + 3], T.rl[:, me, 0:3], "rin")
+    i_pk = V(vec.tensor_copy(T.pk_q[:, 0:SL].bitcast(dt.uint32), T.xq[:, 0:S].bitcast(dt.uint32).indirect(T.co[:, 0:24])))
+    gw(i_pk, "v")
+    send(lambda q: T.pk_q[:, CAP * q:CAP * q + CAP].bitcast(dt.uint8), T.in_q[:, CAP * me:CAP * me + CAP].bitcast(dt.uint8), "q1")
+    gw(a_pk, "a")
+    send(lambda q: T.pk_s[:, CAP * q:CAP * q + CAP], T.in_s[:, CAP * me:CAP * me + CAP], "s1")
+    mine = slice(CAP * me, CAP * me + CAP)
+    sw(i_pk, "v")
+    sw(a_pk, "a")
+    syn.dma_start(T.in_q[:, mine].bitcast(dt.uint8), T.pk_q[:, mine].bitcast(dt.uint8)).then_inc(sem.own1, 16)
+    syn.dma_start(T.in_s[:, mine], T.pk_s[:, mine]).then_inc(sem.own1, 16)
+
+    vw(i_rs)
+    V(vec.tensor_copy(T.rl[:, me, 0:3], T.rs[:, 3 * me:3 * me + 3]))
+    i_own = V(vec.tensor_copy(T.kl[:, me, 0:3], T.ks[:, 3 * me:3 * me + 3]))
+    i_tb = V(vec.memset(T.tab[:], 0.0))
+    vw(6, "gi")
+    i_sv = V(vec.tensor_scalar(T.sv[:], T.sv0[:], T.h192[:, 0:1], None, A.add))
+    aw(max(i_rkl, i_ev, i_od), "v")
+    for c0 in (0, 16):
+        C(act.activation(T.x2[:, c0:c0 + 16:2], T.rk_l[:, 7:64:8], COPY, scale=T.ev[:, 0:1]))
+        a_x2 = C(act.activation(T.x2[:, c0 + 1:c0 + 16:2], T.rk_l[:, 7:64:8], COPY, scale=T.od[:, 0:1]))
+    vw(16, "ld_w")
+    i_wq = V(vec.quantize_mx(T.wq[:], T.ws[:], T.wb[:]))
+    vw(i_own)
+    vw(EACH, "kin")
+    i = V(vec.tensor_tensor(T.ka[:], T.kl[:, 0:4, 0:3], T.kl[:, 4:8, 0:3], A.add))
+    vw(i)
+    i = V(vec.tensor_copy(T.kofs[:], T.ka[:]))
+    vw(a_x2, "a")
+    i_f = V(vec.transpose(T.x2t[:], T.x2[:]))
+    vw(max(i, i_sv, i_tb))
+    i_tab = V(vec.tensor_copy(T.tab[:, 0:TAB].indirect(T.kofs[:, 0:12]), T.sv[:]))
+    vw(i_f)
+    i_f = V(vec.tensor_tensor(T.fof[:], T.x2t[:, 0:16], T.x2t[:, 16:32], A.add))
+    vw(EACH, "rin")
+    V(vec.tensor_copy(T.rofs[:, 0:48:2], T.rl[:, :, 0:3]))
+    i_ro = V(vec.tensor_copy(T.rofs[:, 1:48:2], T.rl[:, :, 0:3]))
+    vw(i_f)
+    i_fo = V(vec.tensor_scalar(T.fo[:], T.fof[:], float(HALF), None, A.add))
+    aw(max(i_ro, i_tab), "v")
+    a_g = C(act.activation(T.d_s[:, SL:2 * SL], T.tab[:, 0:TAB].indirect(T.rofs[:, 24:48]), COPY))
+    vw(max(i_ro, i_tab))
+    i = V(vec.tensor_copy(T.d_s[:, 0:SL], T.tab[:, 0:TAB].indirect(T.rofs[:, 0:24])))
+    vw(i)
+    vw(a_g, "a")
+    i = V(vec.transpose(T.t_s[:], T.d_s[:]))
+    vw(i)
+    i = V(vec.tensor_tensor(T.sg[:], T.t_s[:, 0:2 * SL:32], T.t_s[:, 16:2 * SL:32], A.add))
+    vw(i)
+    i_so = V(vec.tensor_scalar(T.so[:], T.sg[:], float(HALF), None, A.add))
+
+    vw(i_so)
+    vw(32, "own1")
+    vw(EACH, "q1")
+    i_p2 = V(vec.tensor_copy(T.p2_q[:, 0:SL].bitcast(dt.uint32), T.in_q[:, 0:SL].bitcast(dt.uint32).indirect(T.so[:, 0:24])))
+    aw(i_so, "v")
+    aw(32, "own1")
+    aw(EACH, "s1")
+    a_p2 = C(act.activation(T.p2_s[:, 0:SL], T.in_s[:, 0:SL].indirect(T.so[:, 0:24]), COPY))
+    gw(i_p2, "v")
+    send(lambda q: T.p2_q[:, CAP * q:CAP * q + CAP].bitcast(dt.uint8), T.bk_q[:, CAP * me:CAP * me + CAP].bitcast(dt.uint8), "q2")
+    gw(a_p2, "a")
+    send(lambda q: T.p2_s[:, CAP * q:CAP * q + CAP], T.bk_s[:, CAP * me:CAP * me + CAP], "s2")
+    sw(i_p2, "v")
+    sw(a_p2, "a")
+    syn.dma_start(T.bk_q[:, mine].bitcast(dt.uint8), T.p2_q[:, mine].bitcast(dt.uint8)).then_inc(sem.own2, 16)
+    syn.dma_start(T.bk_s[:, mine], T.p2_s[:, mine]).then_inc(sem.own2, 16)
+
+    vw(i_fo)
+    vw(32, "own2")
+    vw(EACH, "q2")
+    aw(i_fo, "v")
+    aw(32, "own2")
+    aw(EACH, "s2")
+    done = []
+    for f in range(2):
+        c = slice(128 * f, 128 * f + 128)
+        off = T.fo[:, 8 * f:8 * f + 8]
+        iv = V(vec.tensor_copy(T.fp_q[:, c].bitcast(dt.uint32), T.bk_q[:, 0:SL].bitcast(dt.uint32).indirect(off)))
+        ia = C(act.activation(T.fp_s[:, c], T.bk_s[:, 0:SL].indirect(off), COPY))
+        done.append((iv, ia))
+    for f in range(2):
+        c = slice(128 * f, 128 * f + 128)
+        W(ten, "t", "v", done[f][0])
+        W(ten, "t", "a", done[f][1])
+        for o in range(O):
+            ws = slice(128 * o, 128 * o + 128)
+            b0 = 512 * (O * f + o)
+            ten.matmul_mx(T.ps[:, b0:b0 + 128], T.wq[:, ws], T.ws[:, ws], T.fp_q[:, c], T.fp_s[:, c], True, True).then_inc(sem.t, 1)
+    for f in range(2):
+        vw(O * f + 1, "t")
+        iv = V(vec.tensor_copy(T.yb[:, 128 * f:128 * f + 128], T.ps[:, 1024 * f:1024 * f + 128]))
+        aw(O * f + 2, "t")
+        ia = C(act.activation(T.yb[:, S + 128 * f:S + 128 * f + 128], T.ps[:, 1024 * f + 512:1024 * f + 640], COPY))
+    sw(iv, "v")
+    syn.dma_start(T.y[:, 0:S], T.yb[:, 0:S]).then_inc(sem.st, 16)
+    aw(ia)
+    act.dma_start(T.y[:, S:2 * S], T.yb[:, S:2 * S]).then_inc(sem.st, 16)
+    sw(32, "st")
+    gw(6 * EACH, "out")

@@ -4,6 +4,7 @@ from concourse.mybir import dt, AluOpType, ActivationFunctionType
 N, S, CAP, K, O = 8, 256, 48, 1024, 2
 SL = N * CAP
 HALF = SL // 2
+RL = N * 64
 TAB = K + SL
 F8, F32, BF, I32, U16 = "float8_e4m3fn_x4", "float32", "bfloat16", "int32", "uint16"
 
@@ -14,21 +15,21 @@ SCRATCH = {
     "kx": ("sbuf", [128, 64], I32), "ko": ("sbuf", [128, 64], I32), "kt": ("sbuf", [128, 64], I32),
     "kf": ("sbuf", [128, 256], I32), "pl": ("sbuf", [128, 256], I32),
     "pio": ("sbuf", [128, 4], I32), "two": ("sbuf", [128, 4], I32), "kf0": ("sbuf", [128, 128], I32),
-    "cq": ("sbuf", [128, 64], F32), "m64": ("sbuf", [128, 64], F32), "sv0": ("sbuf", [128, HALF], F32),
-    "sv": ("sbuf", [128, HALF], BF), "hh": ("sbuf", [128, 4], I32), "h3": ("sbuf", [128, 4], I32),
+    "cq": ("sbuf", [128, 64], F32), "m64": ("sbuf", [128, 64], F32), "sv": ("sbuf", [128, SL], BF),
+    "hh": ("sbuf", [128, 4], I32), "h3": ("sbuf", [128, 4], I32),
     "p31": ("sbuf", [128, 4], I32), "c4": ("sbuf", [128, 4], I32), "c64": ("sbuf", [128, 4], U16),
     "ev": ("sbuf", [128, 1], F32), "od": ("sbuf", [128, 1], F32), "h8": ("sbuf", [128, 1], F32),
-    "h192": ("sbuf", [128, 1], F32), "ini": ("sbuf", [128, 1], F32), "zz": ("sbuf", [128, 256], BF),
+    "ini": ("sbuf", [128, 1], F32), "zz": ("sbuf", [128, 256], BF),
     "win_k": ("sbuf", [128, SL], F32), "win_l": ("sbuf", [128, SL], F32),
     "d_k": ("sbuf", [128, 24, 32], "float16"), "t_k": ("sbuf", [128, 24, 32], "float16"),
-    "d_l": ("sbuf", [128, 24, 32], F32), "t_l": ("sbuf", [128, 24, 32], F32),
-    "mn": ("sbuf", [128, 24, 2], F32), "co": ("sbuf", [128, 24], U16),
-    "ks": ("sbuf", [128, 24], F32), "rs": ("sbuf", [128, 24], F32),
+    "t_l": ("sbuf", [128, SL], F32),
+    "mn": ("sbuf", [128, 24, 2], F32), "co": ("sbuf", [128, 24], U16), "co_me": ("sbuf", [128, 4], U16),
+    "ks": ("sbuf", [128, 24], U16), "rsf": ("sbuf", [128, 12], F32), "rs": ("sbuf", [128, 24], U16),
     "x2": ("sbuf", [128, 32], BF), "x2t": ("sbuf", [128, 32], BF), "fof": ("sbuf", [128, 16], F32), "fo": ("sbuf", [128, 16], U16),
-    "kl": ("sbuf", [128, 8, 4], F32), "rl": ("sbuf", [128, 8, 4], F32),
-    "ka": ("sbuf", [128, 4, 3], F32), "kofs": ("sbuf", [128, 12], U16), "rofs": ("sbuf", [128, 48], U16),
-    "tab": ("sbuf", [128, TAB], BF), "d_s": ("sbuf", [128, 2 * SL], BF), "t_s": ("sbuf", [128, 2 * SL], BF),
-    "sg": ("sbuf", [128, 24], F32), "so": ("sbuf", [128, 24], U16),
+    "kin": ("sbuf", [128, 8, 8], U16), "rin": ("sbuf", [128, 8, 8], U16),
+    "kofs": ("sbuf", [128, 24], U16), "rofs": ("sbuf", [128, 32], U16),
+    "tab": ("sbuf", [128, TAB], BF), "d_s": ("sbuf", [128, RL], BF), "t_s": ("sbuf", [128, 8, 64], BF),
+    "so": ("sbuf", [128, 24], U16), "so_me": ("sbuf", [128, 4], U16),
     "pk_q": ("sbuf", [128, SL], F8), "pk_s": ("sbuf", [128, SL], "uint8"),
     "in_q": ("sbuf", [128, SL], F8), "in_s": ("sbuf", [128, SL], "uint8"),
     "p2_q": ("sbuf", [128, SL], F8), "p2_s": ("sbuf", [128, SL], "uint8"),
@@ -44,8 +45,7 @@ for _c in "kl":
     SCRATCH["pr_" + _c] = ("sbuf", [128, 64], F32)
     SCRATCH["rk_" + _c] = ("sbuf", [128, 64], F32)
     SCRATCH["po_" + _c] = ("sbuf", [128, 8], U16)
-SEMAPHORES = ["v", "a", "t", "gi", "ld_x", "ld_w", "ld_t", "ld_k", "ld_l", "kin", "rin", "q1", "s1", "q2", "s2",
-              "own1", "own2", "out", "st"]
+SEMAPHORES = ["v", "a", "t", "gi", "ld_x", "ld_w", "ld_t", "ld_k", "ld_l", "kin", "rin", "q1", "s1", "q2", "s2", "out", "st"]
 
 
 def rank_program(g, core, T, topo):
@@ -55,7 +55,7 @@ def rank_program(g, core, T, topo):
     A = AluOpType
     COPY = ActivationFunctionType.Copy
     vec, act, ten, syn, sem = g.vector, g.scalar, g.tensor, g.sync, T.sem
-    nv, na, seen = [0], [0], {}
+    nv, na, sent, seen = [0], [0], [0], {}
 
     def V(ins):
         ins.then_inc(sem.v, 1)
@@ -103,29 +103,41 @@ def rank_program(g, core, T, topo):
     def send(src, dst, s):
         g.remote_dma_fused([RemoteDMATransfer(dst_ids=[d], dma_engine_mask=m, remote_sem=sem[s], src=src(q), dst=dst)
                             for q, d, m in dests], local_sem=sem.out)
+        sent[0] += EACH
 
-    act.dma_start(T.xb[:], T.x[:]).then_inc(sem.ld_x, 16)
+    def codes(out, win, off):
+        return V(vec.tensor_copy(out.bitcast(dt.uint32), win.bitcast(dt.uint32).indirect(off)))
+
+    def scales(out, win, off):
+        return C(act.activation(out, win.indirect(off), COPY))
+
     i_kx = V(vec.memset(T.kx[:], 0))
     sw(i_kx, "v")
     aw(i_kx, "v")
     for src, c0 in ((T.ky, 0), (T.lk, 32)):
         for b in range(4):
             (syn if b < 2 else act).dma_start(T.kx[32 * b:32 * b + 8, c0:c0 + 32], src[:]).then_inc(sem.ld_t, 16)
+    act.dma_start(T.xb[:], T.x[:]).then_inc(sem.ld_x, 16)
 
-    g.iota(T.kf0[:], [[16, 8], [128, 16]], 0, 0).then_inc(sem.gi, 1)
-    g.iota(T.pio[:], [[0, 4]], 0, 1).then_inc(sem.gi, 1)
-    g.iota(T.two[:], [[2, 4]], 0, 0).then_inc(sem.gi, 1)
-    g.iota(T.cq[:], [[0, 8], [1, 8]], 0, 0, allow_small_or_imprecise_dtypes=True).then_inc(sem.gi, 1)
-    g.iota(T.win_k[:], [[0, 8], [1, CAP]], K + CAP * me, 0, allow_small_or_imprecise_dtypes=True).then_inc(sem.gi, 1)
-    g.iota(T.sv0[:], [[1, HALF]], -HALF, 0, allow_small_or_imprecise_dtypes=True).then_inc(sem.gi, 1)
+    def iota(ap, pattern, base, cm=0, small=True):
+        (g.iota(ap, pattern, base, cm, allow_small_or_imprecise_dtypes=True) if small else g.iota(ap, pattern, base, cm)).then_inc(sem.gi, 1)
+    iota(T.pio[:], [[0, 4]], 0, 1, small=False)
+    iota(T.kf0[:], [[16, 8], [128, 16]], 0, small=False)
+    iota(T.two[:], [[2, 4]], 0, small=False)
+    iota(T.cq[:], [[0, 8], [1, 8]], 0)
+    iota(T.win_k[:], [[0, 8], [1, CAP]], K + CAP * me)
+    iota(T.win_l[:], [[0, SL]], K)
+    iota(T.sv[:], [[1, SL]], -HALF)
+    i_zz = V(vec.memset(T.zz[:], 0.0))
     V(vec.memset(T.kf[:, 128:256], 0))
-    vw(2, "gi")
+    vw(1, "gi")
     i_hh = V(vec.tensor_scalar(T.hh[:], T.pio[:], 4, 1, A.logical_shift_right, A.bitwise_and))
-    i_h3 = V(vec.tensor_scalar(T.h3[:], T.pio[:], 3, 1, A.logical_shift_right, A.bitwise_and))
+    V(vec.tensor_scalar(T.h3[:], T.pio[:], 3, 1, A.logical_shift_right, A.bitwise_and))
     i_31 = V(vec.tensor_scalar(T.p31[:], T.pio[:], 31, None, A.bitwise_and))
     vw(i_hh)
     i_h8 = V(vec.tensor_scalar(T.h8[:], T.hh[:, 0:1], 8.0, None, A.mult))
     vw(i_h8)
+    vw(2, "gi")
     i_kf = V(vec.tensor_scalar(T.kf[:, 0:128], T.kf0[:], T.h8[:, 0:1], None, A.add))
     sw(i_kf, "v")
     aw(i_kf, "v")
@@ -135,21 +147,19 @@ def rank_program(g, core, T, topo):
                 p = 32 * b + 16 * h + 1
                 (syn if b < 2 else act).dma_start(T.kf[p:p + 1, c0:c0 + 128], src[h:16:2, :]).then_inc(sem[s], 16)
     syn.dma_start(T.wb[:], T.w[:]).then_inc(sem.ld_w, 16)
+    aw(i_zz, "v")
+    for c0 in range(0, TAB, 256):
+        a_tab = C(act.activation(T.tab[:, c0:min(TAB, c0 + 256)], T.zz[:, 0:min(256, TAB - c0)], COPY))
     vw(3, "gi")
     vw(i_31)
     i = V(vec.tensor_tensor(T.c4[:], T.h3[:], T.two[:], A.add))
-    i_ini = V(vec.tensor_scalar(T.ini[:], T.p31[:, 0:1], 12.0, -193.0, A.mult, A.add))
-    i_od = V(vec.tensor_copy(T.od[:], T.hh[:, 0:1]))
-    i_ev = V(vec.tensor_scalar(T.ev[:], T.hh[:, 0:1], -1.0, 1.0, A.mult, A.add))
-    vw(i)
-    i_c64 = V(vec.tensor_copy(T.c64[:], T.c4[:]))
-    vw(4, "gi")
-    i_m64 = V(vec.tensor_scalar(T.m64[:], T.cq[:], 1.0, None, A.min))
+    V(vec.tensor_scalar(T.ini[:], T.p31[:, 0:1], float(CAP // 4), float(-HALF - 1), A.mult, A.add))
     V(vec.memset(T.e_k[:], 0.0))
     V(vec.memset(T.e_l[:], 0.0))
-    V(vec.memset(T.zz[:], 0.0))
-    V(vec.tensor_scalar(T.h192[:], T.hh[:, 0:1], float(HALF), None, A.mult))
-    i_con = V(vec.memset(T.win_l[:], float(K)))
+    vw(i)
+    V(vec.tensor_copy(T.c64[:], T.c4[:]))
+    vw(4, "gi")
+    i_con = V(vec.tensor_scalar(T.m64[:], T.cq[:], 1.0, None, A.min))
 
     vw(i_con)
     vw(128, "ld_t")
@@ -176,127 +186,126 @@ def rank_program(g, core, T, topo):
     for c in kl:
         vw(last[c])
         last[c] = V(vec.tensor_tensor_scan(T["rk_" + c][:], T.m64[:], T["pr_" + c][:], 0.0, A.mult, A.add))
-    vw(128, "ld_k")
-    i_plk = V(vec.tensor_scalar(T.pl[:, 0:128], T.kf[:, 0:128], 3, K - 1, A.logical_shift_right, A.bitwise_and))
     i_rkl = last["l"]
+    vw(128, "ld_k")
+    V(vec.tensor_scalar(T.pl[:, 0:128], T.kf[:, 0:128], 3, K - 1, A.logical_shift_right, A.bitwise_and))
     for c in kl:
         vw(last[c])
         last[c] = V(vec.tensor_scalar(T["po_" + c][:], T["rk_" + c][:, 7:64:8], float(HALF), None, A.add))
-    vw(128, "ld_l")
-    i_pll = V(vec.tensor_scalar(T.pl[:, 128:256], T.kf[:, 128:256], 3, K - 1, A.logical_shift_right, A.bitwise_and))
 
     vw(5, "gi")
-    vw(last["k"])
+    vw(last["l"])
     i_sk = V(vec.tensor_copy(T.win_k[:, 0:SL].indirect(T.po_k[:, 0:8]), T.pl[:, 0:128]))
-    vw(i_pll)
-    i_sl = V(vec.tensor_copy(T.win_l[:, 0:SL].indirect(T.po_l[:, 0:8]), T.pl[:, 128:256]))
-    aw(i_sl, "v")
-    C(act.activation(T.d_l[:, :, 0:16], T.win_l[:], COPY))
-    a_dl = C(act.activation(T.d_l[:, :, 16:32], T.win_l[:], COPY))
+    vw(128, "ld_l")
+    i_pll = V(vec.tensor_scalar(T.pl[:, 128:256], T.kf[:, 128:256], 3, K - 1, A.logical_shift_right, A.bitwise_and))
     vw(i_sk)
     i = V(vec.tensor_copy(T.d_k[:, :, 0:16], T.win_k[:]))
+    vw(16, "ld_x")
+    i_xq = V(vec.quantize_mx(T.xq[:], T.xs[:], T.xb[:]))
     vw(i)
     i = V(vec.tensor_copy(T.d_k[:, :, 16:32], T.d_k[:, :, 0:16]))
     vw(i)
     i = V(vec.transpose(T.t_k[:], T.d_k[:]))
     vw(i)
-    i = V(vec.tensor_tensor(T.mn[:], T.t_k[:, :, 0:2], T.t_k[:, :, 16:18], A.min))
-    vw(i)
-    i_ks = V(vec.tensor_scalar(T.ks[:], T.mn[:, :, 1], (T.ev if me < N // 2 else T.od)[:, 0:1], None, A.mult))
-    i_co = V(vec.tensor_scalar(T.co[:], T.mn[:, :, 0], float(S - 1), None, A.min))
+    i_mn = V(vec.tensor_tensor(T.mn[:], T.t_k[:, :, 0:2], T.t_k[:, :, 16:18], A.min))
+    vw(i_mn)
+    i_ks = V(vec.tensor_copy(T.ks[:], T.mn[:, :, 1]))
     gw(i_ks, "v")
-    send(lambda q: T.ks[:, 3 * q:3 * q + 3], T.kl[:, me, 0:3], "kin")
-    vw(16, "ld_x")
-    i_xq = V(vec.quantize_mx(T.xq[:], T.xs[:], T.xb[:]))
-    vw(a_dl, "a")
-    i = V(vec.transpose(T.t_l[:], T.d_l[:]))
-    aw(i_xq, "v")
-    a_pk = C(act.activation(T.pk_s[:, 0:SL], T.xs[:, 0:S].indirect(T.co[:, 0:24]), COPY))
-    vw(i)
-    i_rs = V(vec.tensor_tensor(T.rs[:], T.t_l[:, :, 1], T.t_l[:, :, 17], A.min))
-    gw(i_rs, "v")
-    send(lambda q: T.rs[:, 3 * q:3 * q + 3], T.rl[:, me, 0:3], "rin")
-    i_pk = V(vec.tensor_copy(T.pk_q[:, 0:SL].bitcast(dt.uint32), T.xq[:, 0:S].bitcast(dt.uint32).indirect(T.co[:, 0:24])))
-    gw(i_pk, "v")
-    send(lambda q: T.pk_q[:, CAP * q:CAP * q + CAP].bitcast(dt.uint8), T.in_q[:, CAP * me:CAP * me + CAP].bitcast(dt.uint8), "q1")
-    gw(a_pk, "a")
-    send(lambda q: T.pk_s[:, CAP * q:CAP * q + CAP], T.in_s[:, CAP * me:CAP * me + CAP], "s1")
-    mine = slice(CAP * me, CAP * me + CAP)
-    sw(i_pk, "v")
-    sw(a_pk, "a")
-    syn.dma_start(T.in_q[:, mine].bitcast(dt.uint8), T.pk_q[:, mine].bitcast(dt.uint8)).then_inc(sem.own1, 16)
-    syn.dma_start(T.in_s[:, mine], T.pk_s[:, mine]).then_inc(sem.own1, 16)
+    send(lambda q: T.ks[:, 3 * q:3 * q + 3], T.kin[:, me, 0:3], "kin")
+    i_co = V(vec.tensor_scalar(T.co[:], T.mn[:, :, 0], float(S - 1), None, A.min))
 
-    vw(i_rs)
-    V(vec.tensor_copy(T.rl[:, me, 0:3], T.rs[:, 3 * me:3 * me + 3]))
-    i_own = V(vec.tensor_copy(T.kl[:, me, 0:3], T.ks[:, 3 * me:3 * me + 3]))
-    i_tb = V(vec.memset(T.tab[:], 0.0))
     vw(6, "gi")
-    i_sv = V(vec.tensor_scalar(T.sv[:], T.sv0[:], T.h192[:, 0:1], None, A.add))
-    aw(max(i_rkl, i_ev, i_od), "v")
+    vw(i_pll)
+    i = V(vec.tensor_copy(T.win_l[:, 0:SL].indirect(T.po_l[:, 0:8]), T.pl[:, 128:256]))
+    vw(i)
+    i = V(vec.transpose(T.t_l[:], T.win_l[:]))
+    vw(i)
+    i = V(vec.tensor_tensor(T.rsf[:], T.t_l[:, 1:SL:32], T.t_l[:, 17:SL:32], A.min))
+    vw(i)
+    V(vec.tensor_copy(T.rs[:, 0:24:2], T.rsf[:]))
+    i_rs = V(vec.tensor_copy(T.rs[:, 1:24:2], T.rsf[:]))
+    gw(i_rs, "v")
+    send(lambda q: T.rs[:, 3 * q - q % 2:3 * q - q % 2 + 4], T.rin[:, me, 0:4], "rin")
+
+    mine = slice(CAP * me, CAP * me + CAP)
+    aw(max(i_xq, i_co), "v")
+    a_pk = scales(T.pk_s[:, 0:SL], T.xs[:, 0:S], T.co[:, 0:24])
+    i_pk = codes(T.pk_q[:, 0:SL], T.xq[:, 0:S], T.co[:, 0:24])
+    gw(a_pk, "a")
+    send(lambda q: T.pk_s[:, CAP * q:CAP * q + CAP], T.in_s[:, mine], "s1")
+    gw(i_pk, "v")
+    send(lambda q: T.pk_q[:, CAP * q:CAP * q + CAP].bitcast(dt.uint8), T.in_q[:, mine].bitcast(dt.uint8), "q1")
+
+    i = V(vec.tensor_scalar(T.co_me[:, 0:3], T.mn[:, 3 * me:3 * me + 3, 0], float(S - 1), None, A.min))
+    V(vec.tensor_copy(T.kin[:, me, 0:3], T.ks[:, 3 * me:3 * me + 3]))
+    V(vec.tensor_copy(T.od[:], T.hh[:, 0:1]))
+    i_ev = V(vec.tensor_scalar(T.ev[:], T.hh[:, 0:1], -1.0, 1.0, A.mult, A.add))
+    vw(i_rs)
+    i_own = V(vec.tensor_copy(T.rin[:, me, 0:4], T.rs[:, 3 * me - me % 2:3 * me - me % 2 + 4]))
+    aw(max(i_ev, i_rkl), "v")
+    a_own = scales(T.in_s[:, mine], T.xs[:, 0:S], T.co_me[:, 0:3])
     for c0 in (0, 16):
         C(act.activation(T.x2[:, c0:c0 + 16:2], T.rk_l[:, 7:64:8], COPY, scale=T.ev[:, 0:1]))
         a_x2 = C(act.activation(T.x2[:, c0 + 1:c0 + 16:2], T.rk_l[:, 7:64:8], COPY, scale=T.od[:, 0:1]))
-    vw(16, "ld_w")
-    i_wq = V(vec.quantize_mx(T.wq[:], T.ws[:], T.wb[:]))
+    vw(i)
+    i_own1 = codes(T.in_q[:, mine], T.xq[:, 0:S], T.co_me[:, 0:3])
+
+    vw(7, "gi")
+    vw(a_tab, "a")
     vw(i_own)
     vw(EACH, "kin")
-    i = V(vec.tensor_tensor(T.ka[:], T.kl[:, 0:4, 0:3], T.kl[:, 4:8, 0:3], A.add))
+    i = V(vec.tensor_copy(T.kofs[:], T.kin[:, :, 0:3]))
     vw(i)
-    i = V(vec.tensor_copy(T.kofs[:], T.ka[:]))
-    vw(a_x2, "a")
-    i_f = V(vec.transpose(T.x2t[:], T.x2[:]))
-    vw(max(i, i_sv, i_tb))
-    i_tab = V(vec.tensor_copy(T.tab[:, 0:TAB].indirect(T.kofs[:, 0:12]), T.sv[:]))
-    vw(i_f)
-    i_f = V(vec.tensor_tensor(T.fof[:], T.x2t[:, 0:16], T.x2t[:, 16:32], A.add))
+    i_tab = V(vec.tensor_copy(T.tab[:, 0:TAB].indirect(T.kofs[:, 0:24]), T.sv[:]))
     vw(EACH, "rin")
-    V(vec.tensor_copy(T.rofs[:, 0:48:2], T.rl[:, :, 0:3]))
-    i_ro = V(vec.tensor_copy(T.rofs[:, 1:48:2], T.rl[:, :, 0:3]))
-    vw(i_f)
-    i_fo = V(vec.tensor_scalar(T.fo[:], T.fof[:], float(HALF), None, A.add))
-    aw(max(i_ro, i_tab), "v")
-    a_g = C(act.activation(T.d_s[:, SL:2 * SL], T.tab[:, 0:TAB].indirect(T.rofs[:, 24:48]), COPY))
-    vw(max(i_ro, i_tab))
-    i = V(vec.tensor_copy(T.d_s[:, 0:SL], T.tab[:, 0:TAB].indirect(T.rofs[:, 0:24])))
+    i = V(vec.tensor_copy(T.rofs[:], T.rin[:, :, 0:4]))
+    aw(i, "v")
+    a_g = C(act.activation(T.d_s[:, RL // 2:RL], T.tab[:, 0:TAB].indirect(T.rofs[:, 16:32]), COPY))
+    vw(i)
+    i = V(vec.tensor_copy(T.d_s[:, 0:RL // 2], T.tab[:, 0:TAB].indirect(T.rofs[:, 0:16])))
     vw(i)
     vw(a_g, "a")
     i = V(vec.transpose(T.t_s[:], T.d_s[:]))
     vw(i)
-    i = V(vec.tensor_tensor(T.sg[:], T.t_s[:, 0:2 * SL:32], T.t_s[:, 16:2 * SL:32], A.add))
-    vw(i)
-    i_so = V(vec.tensor_scalar(T.so[:], T.sg[:], float(HALF), None, A.add))
+    m0 = 16 * (me % 2)
+    i_so = V(vec.tensor_scalar(T.so[:], T.t_s[:, :, m0:m0 + 48:16], float(HALF), None, A.add))
 
     vw(i_so)
-    vw(32, "own1")
+    vw(a_own, "a")
     vw(EACH, "q1")
-    i_p2 = V(vec.tensor_copy(T.p2_q[:, 0:SL].bitcast(dt.uint32), T.in_q[:, 0:SL].bitcast(dt.uint32).indirect(T.so[:, 0:24])))
-    aw(i_so, "v")
-    aw(32, "own1")
+    aw(max(i_so, i_own1), "v")
+    aw(a_own)
     aw(EACH, "s1")
-    a_p2 = C(act.activation(T.p2_s[:, 0:SL], T.in_s[:, 0:SL].indirect(T.so[:, 0:24]), COPY))
+    i_p2 = codes(T.p2_q[:, 0:SL], T.in_q[:, 0:SL], T.so[:, 0:24])
+    a_p2 = scales(T.p2_s[:, 0:SL], T.in_s[:, 0:SL], T.so[:, 0:24])
     gw(i_p2, "v")
-    send(lambda q: T.p2_q[:, CAP * q:CAP * q + CAP].bitcast(dt.uint8), T.bk_q[:, CAP * me:CAP * me + CAP].bitcast(dt.uint8), "q2")
+    send(lambda q: T.p2_q[:, CAP * q:CAP * q + CAP].bitcast(dt.uint8), T.bk_q[:, mine].bitcast(dt.uint8), "q2")
     gw(a_p2, "a")
-    send(lambda q: T.p2_s[:, CAP * q:CAP * q + CAP], T.bk_s[:, CAP * me:CAP * me + CAP], "s2")
-    sw(i_p2, "v")
-    sw(a_p2, "a")
-    syn.dma_start(T.bk_q[:, mine].bitcast(dt.uint8), T.p2_q[:, mine].bitcast(dt.uint8)).then_inc(sem.own2, 16)
-    syn.dma_start(T.bk_s[:, mine], T.p2_s[:, mine]).then_inc(sem.own2, 16)
+    send(lambda q: T.p2_s[:, CAP * q:CAP * q + CAP], T.bk_s[:, mine], "s2")
+    i_sm = V(vec.tensor_scalar(T.so_me[:, 0:3], T.t_s[:, me, m0:m0 + 48:16], float(HALF), None, A.add))
+    vw(i_sm)
+    i_own2 = codes(T.bk_q[:, mine], T.in_q[:, 0:SL], T.so_me[:, 0:3])
+    aw(i_sm, "v")
+    a_own2 = scales(T.bk_s[:, mine], T.in_s[:, 0:SL], T.so_me[:, 0:3])
+    vw(16, "ld_w")
+    V(vec.quantize_mx(T.wq[:], T.ws[:], T.wb[:]))
+    vw(a_x2, "a")
+    i = V(vec.transpose(T.x2t[:], T.x2[:]))
+    vw(i)
+    i = V(vec.tensor_tensor(T.fof[:], T.x2t[:, 0:16], T.x2t[:, 16:32], A.add))
+    vw(i)
+    i_fo = V(vec.tensor_scalar(T.fo[:], T.fof[:], float(HALF), None, A.add))
 
-    vw(i_fo)
-    vw(32, "own2")
+    vw(max(i_own2, i_fo))
     vw(EACH, "q2")
     aw(i_fo, "v")
-    aw(32, "own2")
+    aw(a_own2)
     aw(EACH, "s2")
     done = []
     for f in range(2):
         c = slice(128 * f, 128 * f + 128)
         off = T.fo[:, 8 * f:8 * f + 8]
-        iv = V(vec.tensor_copy(T.fp_q[:, c].bitcast(dt.uint32), T.bk_q[:, 0:SL].bitcast(dt.uint32).indirect(off)))
-        ia = C(act.activation(T.fp_s[:, c], T.bk_s[:, 0:SL].indirect(off), COPY))
-        done.append((iv, ia))
+        done.append((codes(T.fp_q[:, c], T.bk_q[:, 0:SL], off), scales(T.fp_s[:, c], T.bk_s[:, 0:SL], off)))
     for f in range(2):
         c = slice(128 * f, 128 * f + 128)
         W(ten, "t", "v", done[f][0])
@@ -315,4 +324,4 @@ def rank_program(g, core, T, topo):
     aw(ia)
     act.dma_start(T.y[:, S:2 * S], T.yb[:, S:2 * S]).then_inc(sem.st, 16)
     sw(32, "st")
-    gw(6 * EACH, "out")
+    gw(sent[0], "out")

from concourse.bass import DstId, RemoteDMATransfer
from concourse.mybir import dt, AluOpType, ActivationFunctionType

N, S, CAP, K, O = 8, 256, 48, 1024, 2
SL = N * CAP
HALF = SL // 2
RL = N * 64
TAB = K + SL
F8, F32, BF, I32, U16 = "float8_e4m3fn_x4", "float32", "bfloat16", "int32", "uint16"

SCRATCH = {
    "xb": ("sbuf", [128, 4 * S], BF), "wb": ("sbuf", [128, 512 * O], BF),
    "xq": ("sbuf", [128, S], F8), "xs": ("sbuf", [128, S], "uint8"),
    "wq": ("sbuf", [128, 128 * O], F8), "ws": ("sbuf", [128, 128 * O], "uint8"),
    "kx": ("sbuf", [128, 64], I32), "ko": ("sbuf", [128, 64], I32), "kt": ("sbuf", [128, 64], I32),
    "kf": ("sbuf", [128, 256], I32), "pl": ("sbuf", [128, 256], I32),
    "pio": ("sbuf", [128, 4], I32), "two": ("sbuf", [128, 4], I32), "kf0": ("sbuf", [128, 128], I32),
    "cq": ("sbuf", [128, 64], F32), "m64": ("sbuf", [128, 64], F32), "sv": ("sbuf", [128, SL], BF),
    "hh": ("sbuf", [128, 4], I32), "h3": ("sbuf", [128, 4], I32),
    "p31": ("sbuf", [128, 4], I32), "c4": ("sbuf", [128, 4], I32), "c64": ("sbuf", [128, 4], U16),
    "ev": ("sbuf", [128, 1], F32), "od": ("sbuf", [128, 1], F32), "h8": ("sbuf", [128, 1], F32),
    "ini": ("sbuf", [128, 1], F32), "zz": ("sbuf", [128, 256], BF),
    "win_k": ("sbuf", [128, SL], F32), "win_l": ("sbuf", [128, SL], F32),
    "d_k": ("sbuf", [128, 24, 32], "float16"), "t_k": ("sbuf", [128, 24, 32], "float16"),
    "t_l": ("sbuf", [128, SL], F32),
    "mn": ("sbuf", [128, 24, 2], F32), "co": ("sbuf", [128, 24], U16), "co_me": ("sbuf", [128, 4], U16),
    "ks": ("sbuf", [128, 24], U16), "rsf": ("sbuf", [128, 12], F32), "rs": ("sbuf", [128, 24], U16),
    "x2": ("sbuf", [128, 32], BF), "x2t": ("sbuf", [128, 32], BF), "fof": ("sbuf", [128, 16], F32), "fo": ("sbuf", [128, 16], U16),
    "kin": ("sbuf", [128, 8, 8], U16), "rin": ("sbuf", [128, 8, 8], U16),
    "kofs": ("sbuf", [128, 24], U16), "rofs": ("sbuf", [128, 32], U16),
    "tab": ("sbuf", [128, TAB], BF), "d_s": ("sbuf", [128, RL], BF), "t_s": ("sbuf", [128, 8, 64], BF),
    "so": ("sbuf", [128, 24], U16), "so_me": ("sbuf", [128, 4], U16),
    "pk_q": ("sbuf", [128, SL], F8), "pk_s": ("sbuf", [128, SL], "uint8"),
    "in_q": ("sbuf", [128, SL], F8), "in_s": ("sbuf", [128, SL], "uint8"),
    "p2_q": ("sbuf", [128, SL], F8), "p2_s": ("sbuf", [128, SL], "uint8"),
    "bk_q": ("sbuf", [128, SL], F8), "bk_s": ("sbuf", [128, SL], "uint8"),
    "fp_q": ("sbuf", [128, S], F8), "fp_s": ("sbuf", [128, S], "uint8"),
    "ps": ("psum", [128, 2048], F32), "yb": ("sbuf", [128, S * O], F32),
}
for _c in "kl":
    SCRATCH["e_" + _c] = ("sbuf", [128, 256], BF)
    SCRATCH["ef_" + _c] = ("sbuf", [128, 256], BF)
    SCRATCH["cu_" + _c] = ("sbuf", [128, 256], BF)
    SCRATCH["ct_" + _c] = ("sbuf", [128, 256], BF)
    SCRATCH["pr_" + _c] = ("sbuf", [128, 64], F32)
    SCRATCH["rk_" + _c] = ("sbuf", [128, 64], F32)
    SCRATCH["po_" + _c] = ("sbuf", [128, 8], U16)
SEMAPHORES = ["v", "a", "t", "gi", "ld_x", "ld_w", "ld_t", "ld_k", "ld_l", "kin", "rin", "q1", "s1", "q2", "s2", "out", "st"]


def rank_program(g, core, T, topo):
    me = T.rank_of(core)
    if me is None:
        return
    A = AluOpType
    COPY = ActivationFunctionType.Copy
    vec, act, ten, syn, sem = g.vector, g.scalar, g.tensor, g.sync, T.sem
    nv, na, sent, seen = [0], [0], [0], {}

    def V(ins):
        ins.then_inc(sem.v, 1)
        nv[0] += 1
        return nv[0]

    def C(ins):
        ins.then_inc(sem.a, 1)
        na[0] += 1
        return na[0]

    def W(q, name, s, k):
        if seen.get((name, s), 0) < k:
            q.wait_ge(sem[s], k)
            seen[(name, s)] = k

    def vw(k, s="v"):
        W(vec, "v", s, k)

    def aw(k, s="a"):
        W(act, "a", s, k)

    def sw(k, s):
        W(syn, "s", s, k)

    def gw(k, s):
        W(g, "g", s, k)

    near, far = 0, 0
    dests = []
    for i in range(1, N):
        q = (me + i) % N
        dst = T.cores[q]
        eng = topo.engines(core, dst)
        if topo.die(dst) == topo.die(core):
            pick = eng[0::2][2 * near:2 * near + 2]
            near += 1
        else:
            pick = eng[1::2][2 * far:2 * far + 2]
            far += 1
        rid, pid, _ = topo.addr(dst)
        dests.append((q, DstId(rid=rid, pnc=pid), sum(1 << e for e in pick)))
    EACH = 2 * (N - 1)

    def send(src, dst, s):
        g.remote_dma_fused([RemoteDMATransfer(dst_ids=[d], dma_engine_mask=m, remote_sem=sem[s], src=src(q), dst=dst)
                            for q, d, m in dests], local_sem=sem.out)
        sent[0] += EACH

    def codes(out, win, off):
        return V(vec.tensor_copy(out.bitcast(dt.uint32), win.bitcast(dt.uint32).indirect(off)))

    def scales(out, win, off):
        return C(act.activation(out, win.indirect(off), COPY))

    i_kx = V(vec.memset(T.kx[:], 0))
    sw(i_kx, "v")
    aw(i_kx, "v")
    for src, c0 in ((T.ky, 0), (T.lk, 32)):
        for b in range(4):
            (syn if b < 2 else act).dma_start(T.kx[32 * b:32 * b + 8, c0:c0 + 32], src[:]).then_inc(sem.ld_t, 16)
    act.dma_start(T.xb[:], T.x[:]).then_inc(sem.ld_x, 16)

    def iota(ap, pattern, base, cm=0, small=True):
        (g.iota(ap, pattern, base, cm, allow_small_or_imprecise_dtypes=True) if small else g.iota(ap, pattern, base, cm)).then_inc(sem.gi, 1)
    iota(T.pio[:], [[0, 4]], 0, 1, small=False)
    iota(T.kf0[:], [[16, 8], [128, 16]], 0, small=False)
    iota(T.two[:], [[2, 4]], 0, small=False)
    iota(T.cq[:], [[0, 8], [1, 8]], 0)
    iota(T.win_k[:], [[0, 8], [1, CAP]], K + CAP * me)
    iota(T.win_l[:], [[0, SL]], K)
    iota(T.sv[:], [[1, SL]], -HALF)
    i_zz = V(vec.memset(T.zz[:], 0.0))
    V(vec.memset(T.kf[:, 128:256], 0))
    vw(1, "gi")
    i_hh = V(vec.tensor_scalar(T.hh[:], T.pio[:], 4, 1, A.logical_shift_right, A.bitwise_and))
    V(vec.tensor_scalar(T.h3[:], T.pio[:], 3, 1, A.logical_shift_right, A.bitwise_and))
    i_31 = V(vec.tensor_scalar(T.p31[:], T.pio[:], 31, None, A.bitwise_and))
    vw(i_hh)
    i_h8 = V(vec.tensor_scalar(T.h8[:], T.hh[:, 0:1], 8.0, None, A.mult))
    vw(i_h8)
    vw(2, "gi")
    i_kf = V(vec.tensor_scalar(T.kf[:, 0:128], T.kf0[:], T.h8[:, 0:1], None, A.add))
    sw(i_kf, "v")
    aw(i_kf, "v")
    for src, c0, s in ((T.ky, 0, "ld_k"), (T.lk, 128, "ld_l")):
        for b in range(4):
            for h in range(2):
                p = 32 * b + 16 * h + 1
                (syn if b < 2 else act).dma_start(T.kf[p:p + 1, c0:c0 + 128], src[h:16:2, :]).then_inc(sem[s], 16)
    syn.dma_start(T.wb[:], T.w[:]).then_inc(sem.ld_w, 16)
    aw(i_zz, "v")
    for c0 in range(0, TAB, 256):
        a_tab = C(act.activation(T.tab[:, c0:min(TAB, c0 + 256)], T.zz[:, 0:min(256, TAB - c0)], COPY))
    vw(3, "gi")
    vw(i_31)
    i = V(vec.tensor_tensor(T.c4[:], T.h3[:], T.two[:], A.add))
    V(vec.tensor_scalar(T.ini[:], T.p31[:, 0:1], float(CAP // 4), float(-HALF - 1), A.mult, A.add))
    V(vec.memset(T.e_k[:], 0.0))
    V(vec.memset(T.e_l[:], 0.0))
    vw(i)
    V(vec.tensor_copy(T.c64[:], T.c4[:]))
    vw(4, "gi")
    i_con = V(vec.tensor_scalar(T.m64[:], T.cq[:], 1.0, None, A.min))

    vw(i_con)
    vw(128, "ld_t")
    i = V(vec.tensor_scalar(T.ko[:], T.kx[:], N - 1, None, A.bitwise_and))
    vw(i)
    i = V(vec.transpose(T.kt[:], T.ko[:]))
    vw(i)
    kl = ("k", "l")
    last = {}
    for c, w0 in (("k", 0), ("l", 32)):
        last[c] = V(vec.tensor_tensor(T["e_" + c][:, 0:256:4], T.kt[:, w0:w0 + 8].indirect(T.c64[:, 0:4]), T.cq[:], A.is_equal))
    for c in kl:
        vw(last[c])
        last[c] = V(vec.transpose(T["ef_" + c][:], T["e_" + c][:]))
    for c in kl:
        vw(last[c])
        last[c] = V(vec.tensor_tensor_scan(T["cu_" + c][:], T["ef_" + c][:], T.zz[:], T.ini[:, 0:1], A.add, A.add))
    for c in kl:
        vw(last[c])
        last[c] = V(vec.transpose(T["ct_" + c][:], T["cu_" + c][:]))
    for c in kl:
        vw(last[c])
        last[c] = V(vec.tensor_tensor(T["pr_" + c][:], T["e_" + c][:, 0:256:4], T["ct_" + c][:, 0:256:4], A.mult))
    for c in kl:
        vw(last[c])
        last[c] = V(vec.tensor_tensor_scan(T["rk_" + c][:], T.m64[:], T["pr_" + c][:], 0.0, A.mult, A.add))
    i_rkl = last["l"]
    vw(128, "ld_k")
    V(vec.tensor_scalar(T.pl[:, 0:128], T.kf[:, 0:128], 3, K - 1, A.logical_shift_right, A.bitwise_and))
    for c in kl:
        vw(last[c])
        last[c] = V(vec.tensor_scalar(T["po_" + c][:], T["rk_" + c][:, 7:64:8], float(HALF), None, A.add))

    vw(5, "gi")
    vw(last["l"])
    i_sk = V(vec.tensor_copy(T.win_k[:, 0:SL].indirect(T.po_k[:, 0:8]), T.pl[:, 0:128]))
    vw(128, "ld_l")
    i_pll = V(vec.tensor_scalar(T.pl[:, 128:256], T.kf[:, 128:256], 3, K - 1, A.logical_shift_right, A.bitwise_and))
    vw(i_sk)
    i = V(vec.tensor_copy(T.d_k[:, :, 0:16], T.win_k[:]))
    vw(16, "ld_x")
    i_xq = V(vec.quantize_mx(T.xq[:], T.xs[:], T.xb[:]))
    vw(i)
    i = V(vec.tensor_copy(T.d_k[:, :, 16:32], T.d_k[:, :, 0:16]))
    vw(i)
    i = V(vec.transpose(T.t_k[:], T.d_k[:]))
    vw(i)
    i_mn = V(vec.tensor_tensor(T.mn[:], T.t_k[:, :, 0:2], T.t_k[:, :, 16:18], A.min))
    vw(i_mn)
    i_ks = V(vec.tensor_copy(T.ks[:], T.mn[:, :, 1]))
    gw(i_ks, "v")
    send(lambda q: T.ks[:, 3 * q:3 * q + 3], T.kin[:, me, 0:3], "kin")
    i_co = V(vec.tensor_scalar(T.co[:], T.mn[:, :, 0], float(S - 1), None, A.min))

    vw(6, "gi")
    vw(i_pll)
    i = V(vec.tensor_copy(T.win_l[:, 0:SL].indirect(T.po_l[:, 0:8]), T.pl[:, 128:256]))
    vw(i)
    i = V(vec.transpose(T.t_l[:], T.win_l[:]))
    vw(i)
    i = V(vec.tensor_tensor(T.rsf[:], T.t_l[:, 1:SL:32], T.t_l[:, 17:SL:32], A.min))
    vw(i)
    V(vec.tensor_copy(T.rs[:, 0:24:2], T.rsf[:]))
    i_rs = V(vec.tensor_copy(T.rs[:, 1:24:2], T.rsf[:]))
    gw(i_rs, "v")
    send(lambda q: T.rs[:, 3 * q - q % 2:3 * q - q % 2 + 4], T.rin[:, me, 0:4], "rin")

    mine = slice(CAP * me, CAP * me + CAP)
    aw(max(i_xq, i_co), "v")
    a_pk = scales(T.pk_s[:, 0:SL], T.xs[:, 0:S], T.co[:, 0:24])
    i_pk = codes(T.pk_q[:, 0:SL], T.xq[:, 0:S], T.co[:, 0:24])
    gw(a_pk, "a")
    send(lambda q: T.pk_s[:, CAP * q:CAP * q + CAP], T.in_s[:, mine], "s1")
    gw(i_pk, "v")
    send(lambda q: T.pk_q[:, CAP * q:CAP * q + CAP].bitcast(dt.uint8), T.in_q[:, mine].bitcast(dt.uint8), "q1")

    i = V(vec.tensor_scalar(T.co_me[:, 0:3], T.mn[:, 3 * me:3 * me + 3, 0], float(S - 1), None, A.min))
    V(vec.tensor_copy(T.kin[:, me, 0:3], T.ks[:, 3 * me:3 * me + 3]))
    V(vec.tensor_copy(T.od[:], T.hh[:, 0:1]))
    i_ev = V(vec.tensor_scalar(T.ev[:], T.hh[:, 0:1], -1.0, 1.0, A.mult, A.add))
    vw(i_rs)
    i_own = V(vec.tensor_copy(T.rin[:, me, 0:4], T.rs[:, 3 * me - me % 2:3 * me - me % 2 + 4]))
    aw(max(i_ev, i_rkl), "v")
    a_own = scales(T.in_s[:, mine], T.xs[:, 0:S], T.co_me[:, 0:3])
    for c0 in (0, 16):
        C(act.activation(T.x2[:, c0:c0 + 16:2], T.rk_l[:, 7:64:8], COPY, scale=T.ev[:, 0:1]))
        a_x2 = C(act.activation(T.x2[:, c0 + 1:c0 + 16:2], T.rk_l[:, 7:64:8], COPY, scale=T.od[:, 0:1]))
    vw(i)
    i_own1 = codes(T.in_q[:, mine], T.xq[:, 0:S], T.co_me[:, 0:3])

    vw(7, "gi")
    vw(a_tab, "a")
    vw(i_own)
    vw(EACH, "kin")
    i = V(vec.tensor_copy(T.kofs[:], T.kin[:, :, 0:3]))
    vw(i)
    i_tab = V(vec.tensor_copy(T.tab[:, 0:TAB].indirect(T.kofs[:, 0:24]), T.sv[:]))
    vw(EACH, "rin")
    i = V(vec.tensor_copy(T.rofs[:], T.rin[:, :, 0:4]))
    aw(i, "v")
    a_g = C(act.activation(T.d_s[:, RL // 2:RL], T.tab[:, 0:TAB].indirect(T.rofs[:, 16:32]), COPY))
    vw(i)
    i = V(vec.tensor_copy(T.d_s[:, 0:RL // 2], T.tab[:, 0:TAB].indirect(T.rofs[:, 0:16])))
    vw(i)
    vw(a_g, "a")
    i = V(vec.transpose(T.t_s[:], T.d_s[:]))
    vw(i)
    m0 = 16 * (me % 2)
    i_so = V(vec.tensor_scalar(T.so[:], T.t_s[:, :, m0:m0 + 48:16], float(HALF), None, A.add))

    vw(i_so)
    vw(a_own, "a")
    vw(EACH, "q1")
    aw(max(i_so, i_own1), "v")
    aw(a_own)
    aw(EACH, "s1")
    i_p2 = codes(T.p2_q[:, 0:SL], T.in_q[:, 0:SL], T.so[:, 0:24])
    a_p2 = scales(T.p2_s[:, 0:SL], T.in_s[:, 0:SL], T.so[:, 0:24])
    gw(i_p2, "v")
    send(lambda q: T.p2_q[:, CAP * q:CAP * q + CAP].bitcast(dt.uint8), T.bk_q[:, mine].bitcast(dt.uint8), "q2")
    gw(a_p2, "a")
    send(lambda q: T.p2_s[:, CAP * q:CAP * q + CAP], T.bk_s[:, mine], "s2")
    i_sm = V(vec.tensor_scalar(T.so_me[:, 0:3], T.t_s[:, me, m0:m0 + 48:16], float(HALF), None, A.add))
    vw(i_sm)
    i_own2 = codes(T.bk_q[:, mine], T.in_q[:, 0:SL], T.so_me[:, 0:3])
    aw(i_sm, "v")
    a_own2 = scales(T.bk_s[:, mine], T.in_s[:, 0:SL], T.so_me[:, 0:3])
    vw(16, "ld_w")
    V(vec.quantize_mx(T.wq[:], T.ws[:], T.wb[:]))
    vw(a_x2, "a")
    i = V(vec.transpose(T.x2t[:], T.x2[:]))
    vw(i)
    i = V(vec.tensor_tensor(T.fof[:], T.x2t[:, 0:16], T.x2t[:, 16:32], A.add))
    vw(i)
    i_fo = V(vec.tensor_scalar(T.fo[:], T.fof[:], float(HALF), None, A.add))

    vw(max(i_own2, i_fo))
    vw(EACH, "q2")
    aw(i_fo, "v")
    aw(a_own2)
    aw(EACH, "s2")
    done = []
    for f in range(2):
        c = slice(128 * f, 128 * f + 128)
        off = T.fo[:, 8 * f:8 * f + 8]
        done.append((codes(T.fp_q[:, c], T.bk_q[:, 0:SL], off), scales(T.fp_s[:, c], T.bk_s[:, 0:SL], off)))
    for f in range(2):
        c = slice(128 * f, 128 * f + 128)
        W(ten, "t", "v", done[f][0])
        W(ten, "t", "a", done[f][1])
        for o in range(O):
            ws = slice(128 * o, 128 * o + 128)
            b0 = 512 * (O * f + o)
            ten.matmul_mx(T.ps[:, b0:b0 + 128], T.wq[:, ws], T.ws[:, ws], T.fp_q[:, c], T.fp_s[:, c], True, True).then_inc(sem.t, 1)
    for f in range(2):
        vw(O * f + 1, "t")
        iv = V(vec.tensor_copy(T.yb[:, 128 * f:128 * f + 128], T.ps[:, 1024 * f:1024 * f + 128]))
        aw(O * f + 2, "t")
        ia = C(act.activation(T.yb[:, S + 128 * f:S + 128 * f + 128], T.ps[:, 1024 * f + 512:1024 * f + 640], COPY))
    sw(iv, "v")
    syn.dma_start(T.y[:, 0:S], T.yb[:, 0:S]).then_inc(sem.st, 16)
    aw(ia)
    act.dma_start(T.y[:, S:2 * S], T.yb[:, S:2 * S]).then_inc(sem.st, 16)
    sw(32, "st")
    gw(sent[0], "out")
